import numpy as np
import ml_dtypes


def mxq(x, axis, fmt="e4m3"):
    dtype, down = {"e4m3": (ml_dtypes.float8_e4m3fn, 7), "e5m2": (ml_dtypes.float8_e5m2, 14)}[fmt]
    v = np.moveaxis(np.asarray(x, np.float32).astype(ml_dtypes.bfloat16).astype(np.float64), axis, -1)
    blocks = v.reshape(v.shape[:-1] + (-1, 32))
    amax = np.abs(blocks).max(-1, keepdims=True)
    byte = np.maximum(np.where(amax > 0, np.frexp(amax)[1] - 1 + 127, 0) - down, 1)
    scale = np.exp2(byte - 127.0)
    codes = (blocks / scale).astype(np.float32).astype(dtype).astype(np.float64)
    return np.moveaxis((codes * scale).reshape(v.shape), -1, axis)


WIDE = False


def mx_kscale(k):
    if not WIDE:
        return np.ones(k)
    levels = np.array([10, -10, 5, -5, 0])
    if k % 512:
        return np.exp2(np.random.permutation(np.resize(levels, k // 32))).repeat(32)
    a = np.empty((k // 512, 16))
    for p in range(k // 512):
        a[p, :8] = np.random.permutation(np.resize(levels, 8))
        for g in range(8):
            far = levels[np.abs(levels - a[p, g]) >= 10]
            a[p, g + 8] = far[np.random.randint(len(far))]
    return np.exp2(a.ravel()).repeat(32)


def f64(x):
    return np.asarray(x).astype(np.float64)


def striped(idx):
    return np.tile(idx.reshape(-1, 16).T, (8, 1)).astype(np.uint16)


def unstriped(offs):
    return offs[:16].T.reshape(-1).astype(np.int64)


def pack_weight(w):
    k, n = w.shape
    w = f64(np.asarray(w, np.float32).astype(ml_dtypes.bfloat16)).reshape(k // 32, 32, n)
    amax = np.abs(w).max(1)
    byte = np.clip(np.where(amax > 0, np.frexp(amax)[1] - 1 + 127 - 7, 1), 1, 254)
    scaled = (w * np.exp2(127.0 - byte)[:, None, :]).reshape(k, n).astype(np.float32)
    words = np.ascontiguousarray(scaled.reshape(k // 512, 128, 4, n).transpose(0, 1, 3, 2)).astype(ml_dtypes.float8_e4m3fn).view(np.uint8)
    return words, np.ascontiguousarray(byte.astype(np.uint8).reshape(k // 512, 16, n))


def unpack_weight(words, scales):
    g, p, n, _ = words.shape
    vals = np.ascontiguousarray(words).view(ml_dtypes.float8_e4m3fn).astype(np.float64) * np.repeat(np.exp2(scales.astype(np.float64) - 127.0), 8, axis=1)[..., None]
    return vals.transpose(0, 1, 3, 2).reshape(g * 512, n)


K, T, S, N = 512, 4096, 1024, 128


def setup_inputs():
    n = np.random.standard_normal
    s = mx_kscale(K)[:, None]
    w1, w2 = n((2, K, N)) / np.sqrt(2 * K) / s[None]
    p1, p2 = pack_weight(w1), pack_weight(w2)
    return {
        "xT": (n((K, S)) * s).astype(np.float32),
        "sT": (n((K, T)) * s).astype(np.float32),
        "w1_words": p1[0],
        "w1_scales": p1[1],
        "w2_words": p2[0],
        "w2_scales": p2[1],
        "offs": striped(np.random.permutation(T)[:S]),
    }


def reference(xT, sT, w1_words, w1_scales, w2_words, w2_scales, offs):
    y = unpack_weight(w1_words, w1_scales).T @ mxq(f64(xT), 0, "e4m3") + unpack_weight(w2_words, w2_scales).T @ mxq(f64(sT)[:, unstriped(offs)], 0, "e4m3")
    return y

@@ -1,0 +1,139 @@
+from contextlib import ExitStack
+
+import concourse.mybir as mybir
+
+F32 = mybir.dt.float32
+BF16 = mybir.dt.bfloat16
+I32 = mybir.dt.int32
+U32 = mybir.dt.uint32
+U16 = mybir.dt.uint16
+U8 = mybir.dt.uint8
+FP8X4 = mybir.dt.float8_e4m3fn_x4
+
+P = 128
+PACK = 4
+T = 4096
+S = 1024
+M = 128
+LISTED = 16
+HALF = 512
+BLOCK = 256
+V_COLS = 160
+
+FLOPS = 2 * 2 * 512 * M * S
+
+
+def tile_picked_recall_none_e_kernel(
+    tc, xT, sT, w1_words, w1_scales, w2_words, w2_scales, offs, out
+):
+    nc = tc.nc
+    with ExitStack() as ctx:
+        keep = ctx.enter_context(tc.tile_pool(name="keep", bufs=1))
+        psum = ctx.enter_context(tc.psum_pool(name="psum", bufs=1))
+
+        s_rows = sT.rearrange("(p t) n -> p t n", t=PACK)
+        x_rows = xT.rearrange("(p t) n -> p t n", t=PACK)
+
+        planes = [keep.tile([P, T], F32, name=f"plane{t}") for t in range(PACK)]
+        offsets = keep.tile([P, S // LISTED], U16, name="offsets")
+        nc.sync.dma_start(out=planes[0][:], in_=s_rows[:, 0, :])
+        nc.sync.dma_start(out=offsets[:], in_=offs)
+        w_codes = [keep.tile([P, M], U32, name=f"w_codes{i}", align_bytes=64) for i in range(2)]
+        for codes, words in zip(w_codes, (w1_words, w2_words)):
+            nc.sync.dma_start(out=codes[:].bitcast(I32), in_=words[0].rearrange("p m r -> p (m r)").bitcast(I32))
+        for t in range(1, PACK):
+            nc.sync.dma_start(out=planes[t][:], in_=s_rows[:, t, :])
+        x_raw = []
+        for b in range(S // BLOCK):
+            raw = keep.tile([P, PACK, BLOCK], F32, name=f"x_raw{b}")
+            nc.sync.dma_start(out=raw[:], in_=x_rows[:, :, b * BLOCK : (b + 1) * BLOCK])
+            x_raw.append(raw)
+
+        w_scales = [keep.tile([P, M], U8, name=f"w_scales{i}", align_bytes=64) for i in range(2)]
+        for plane in w_scales:
+            nc.gpsimd.memset(plane[:].bitcast(I32), 0)
+        for plane, scales in zip(w_scales, (w1_scales, w2_scales)):
+            for q in range(4):
+                nc.gpsimd.dma_start(
+                    out=plane[32 * q : 32 * q + 4, :].bitcast(I32),
+                    in_=scales[0, 4 * q : 4 * q + 4, :].bitcast(I32),
+                )
+
+        acc = [psum.tile([P, BLOCK], F32, name=f"acc{b}") for b in range(S // BLOCK)]
+
+        s_packed = [keep.tile([P, HALF, PACK], BF16, name=f"s_packed{h}", align_bytes=64) for h in range(2)]
+        s_codes = [keep.tile([P, HALF], U32, name=f"s_codes{h}", align_bytes=64) for h in range(2)]
+        s_scales = [keep.tile([P, HALF], U8, name=f"s_scales{h}", align_bytes=64) for h in range(2)]
+        x_packed = [keep.tile([P, BLOCK, PACK], BF16, name=f"x_packed{b}", align_bytes=64) for b in range(4)]
+        x_codes = [keep.tile([P, BLOCK], U32, name=f"x_codes{b}", align_bytes=64) for b in range(4)]
+        x_scales = [keep.tile([P, BLOCK], U8, name=f"x_scales{b}", align_bytes=64) for b in range(4)]
+        result = [keep.tile([P, BLOCK], F32, name=f"result{b}") for b in range(4)]
+
+        def gather(t, h):
+            cols = HALF // LISTED
+            nc.vector.tensor_copy(
+                out=s_packed[h][:, :, t], in_=planes[t][:].indirect(offsets[:, h * cols : (h + 1) * cols])
+            )
+
+        def quantize(packed, codes, scales):
+            nc.vector.quantize_mx(
+                out=codes[:].bitcast(FP8X4), scales=scales[:], in_=packed[:].rearrange("p n t -> p (n t)")
+            )
+
+        def memories_times_w2(h):
+            for i in range(HALF // BLOCK):
+                cols = slice(i * BLOCK, (i + 1) * BLOCK)
+                nc.tensor.matmul_mx(
+                    out=acc[h * (HALF // BLOCK) + i][:],
+                    lhsT=w_codes[1][:].bitcast(FP8X4),
+                    lhsT_scale=w_scales[1][:],
+                    rhs=s_codes[h][:, cols].bitcast(FP8X4),
+                    rhs_scale=s_scales[h][:, cols],
+                    start=True,
+                    stop=False,
+                )
+
+        def queries_times_w1(b):
+            nc.tensor.matmul_mx(
+                out=acc[b][:],
+                lhsT=w_codes[0][:].bitcast(FP8X4),
+                lhsT_scale=w_scales[0][:],
+                rhs=x_codes[b][:].bitcast(FP8X4),
+                rhs_scale=x_scales[b][:],
+                start=False,
+                stop=True,
+            )
+
+        def interleave(copy, b, c0, c1):
+            copy(out=x_packed[b][:, c0:c1, :], in_=x_raw[b][:, :, c0:c1].rearrange("p t n -> p n t"))
+
+        def store(b):
+            nc.sync.dma_start(out=out[:, b * BLOCK : (b + 1) * BLOCK], in_=result[b][:])
+
+        for t in range(PACK - 1):
+            for h in range(2):
+                gather(t, h)
+        gather(3, 0)
+        interleave(nc.scalar.copy, 0, 0, BLOCK)
+        quantize(s_packed[0], s_codes[0], s_scales[0])
+        memories_times_w2(0)
+        gather(3, 1)
+        interleave(nc.scalar.copy, 1, 0, BLOCK)
+        quantize(x_packed[0], x_codes[0], x_scales[0])
+        queries_times_w1(0)
+        quantize(s_packed[1], s_codes[1], s_scales[1])
+        memories_times_w2(1)
+        quantize(x_packed[1], x_codes[1], x_scales[1])
+        queries_times_w1(1)
+        interleave(nc.scalar.copy, 2, 0, BLOCK)
+        nc.vector.tensor_copy(out=result[0][:], in_=acc[0][:])
+        store(0)
+        quantize(x_packed[2], x_codes[2], x_scales[2])
+        queries_times_w1(2)
+        interleave(nc.vector.tensor_copy, 3, 0, V_COLS)
+        interleave(nc.scalar.copy, 3, V_COLS, BLOCK)
+        quantize(x_packed[3], x_codes[3], x_scales[3])
+        queries_times_w1(3)
+        for b in range(1, 4):
+            nc.scalar.copy(out=result[b][:], in_=acc[b][:])
+            store(b)

@@ -16,9 +16,7 @@ T = 4096
 S = 1024
 M = 128
 LISTED = 16
-HALF = 512
-BLOCK = 256
-V_COLS = 160
+BLOCKS = ((0, 256), (256, 256), (512, 256), (768, 128), (896, 128))
 
 FLOPS = 2 * 2 * 512 * M * S
 
@@ -41,57 +39,58 @@ def tile_picked_recall_none_e_kernel(
         w_codes = [keep.tile([P, M], U32, name=f"w_codes{i}", align_bytes=64) for i in range(2)]
         for codes, words in zip(w_codes, (w1_words, w2_words)):
             nc.sync.dma_start(out=codes[:].bitcast(I32), in_=words[0].rearrange("p m r -> p (m r)").bitcast(I32))
-        for t in range(1, PACK):
-            nc.sync.dma_start(out=planes[t][:], in_=s_rows[:, t, :])
-        x_raw = []
-        for b in range(S // BLOCK):
-            raw = keep.tile([P, PACK, BLOCK], F32, name=f"x_raw{b}")
-            nc.sync.dma_start(out=raw[:], in_=x_rows[:, :, b * BLOCK : (b + 1) * BLOCK])
-            x_raw.append(raw)
-
+        nc.sync.dma_start(out=planes[1][:], in_=s_rows[:, 1, :])
         w_scales = [keep.tile([P, M], U8, name=f"w_scales{i}", align_bytes=64) for i in range(2)]
         for plane in w_scales:
             nc.gpsimd.memset(plane[:].bitcast(I32), 0)
         for plane, scales in zip(w_scales, (w1_scales, w2_scales)):
             for q in range(4):
-                nc.gpsimd.dma_start(
+                nc.scalar.dma_start(
                     out=plane[32 * q : 32 * q + 4, :].bitcast(I32),
                     in_=scales[0, 4 * q : 4 * q + 4, :].bitcast(I32),
                 )
+        for t in range(2, PACK):
+            nc.sync.dma_start(out=planes[t][:], in_=s_rows[:, t, :])
+        x_raw = []
+        for b, (j0, n) in enumerate(BLOCKS):
+            raw = keep.tile([P, PACK, n], F32, name=f"x_raw{b}")
+            nc.sync.dma_start(out=raw[:], in_=x_rows[:, :, j0 : j0 + n])
+            x_raw.append(raw)
 
-        acc = [psum.tile([P, BLOCK], F32, name=f"acc{b}") for b in range(S // BLOCK)]
+        acc = [psum.tile([P, n], F32, name=f"acc{b}") for b, (j0, n) in enumerate(BLOCKS)]
 
-        s_packed = [keep.tile([P, HALF, PACK], BF16, name=f"s_packed{h}", align_bytes=64) for h in range(2)]
-        s_codes = [keep.tile([P, HALF], U32, name=f"s_codes{h}", align_bytes=64) for h in range(2)]
-        s_scales = [keep.tile([P, HALF], U8, name=f"s_scales{h}", align_bytes=64) for h in range(2)]
-        x_packed = [keep.tile([P, BLOCK, PACK], BF16, name=f"x_packed{b}", align_bytes=64) for b in range(4)]
-        x_codes = [keep.tile([P, BLOCK], U32, name=f"x_codes{b}", align_bytes=64) for b in range(4)]
-        x_scales = [keep.tile([P, BLOCK], U8, name=f"x_scales{b}", align_bytes=64) for b in range(4)]
-        result = [keep.tile([P, BLOCK], F32, name=f"result{b}") for b in range(4)]
+        s_packed = keep.tile([P, S, PACK], BF16, align_bytes=64)
+        s_codes = keep.tile([P, S], U32, align_bytes=64)
+        s_scales = keep.tile([P, S], U8, align_bytes=64)
+        x_packed = [keep.tile([P, n, PACK], BF16, name=f"x_packed{b}", align_bytes=64) for b, (j0, n) in enumerate(BLOCKS)]
+        x_codes = [keep.tile([P, n], U32, name=f"x_codes{b}", align_bytes=64) for b, (j0, n) in enumerate(BLOCKS)]
+        x_scales = [keep.tile([P, n], U8, name=f"x_scales{b}", align_bytes=64) for b, (j0, n) in enumerate(BLOCKS)]
+        result = [keep.tile([P, n], F32, name=f"result{b}") for b, (j0, n) in enumerate(BLOCKS)]
 
-        def gather(t, h):
-            cols = HALF // LISTED
-            nc.vector.tensor_copy(
-                out=s_packed[h][:, :, t], in_=planes[t][:].indirect(offsets[:, h * cols : (h + 1) * cols])
-            )
+        def gather(t):
+            nc.vector.tensor_copy(out=s_packed[:, :, t], in_=planes[t][:].indirect(offsets[:]))
 
         def quantize(packed, codes, scales):
-            nc.vector.quantize_mx(
-                out=codes[:].bitcast(FP8X4), scales=scales[:], in_=packed[:].rearrange("p n t -> p (n t)")
-            )
+            nc.vector.quantize_mx(out=codes.bitcast(FP8X4), scales=scales, in_=packed.rearrange("p n t -> p (n t)"))
 
-        def memories_times_w2(h):
-            for i in range(HALF // BLOCK):
-                cols = slice(i * BLOCK, (i + 1) * BLOCK)
-                nc.tensor.matmul_mx(
-                    out=acc[h * (HALF // BLOCK) + i][:],
-                    lhsT=w_codes[1][:].bitcast(FP8X4),
-                    lhsT_scale=w_scales[1][:],
-                    rhs=s_codes[h][:, cols].bitcast(FP8X4),
-                    rhs_scale=s_scales[h][:, cols],
-                    start=True,
-                    stop=False,
-                )
+        def quantize_queries(b):
+            quantize(x_packed[b][:], x_codes[b][:], x_scales[b][:])
+
+        def quantize_memories(j0, j1):
+            quantize(s_packed[:, j0:j1, :], s_codes[:, j0:j1], s_scales[:, j0:j1])
+
+        def memories_times_w2(b):
+            j0, n = BLOCKS[b]
+            cols = slice(j0, j0 + n)
+            nc.tensor.matmul_mx(
+                out=acc[b][:],
+                lhsT=w_codes[1][:].bitcast(FP8X4),
+                lhsT_scale=w_scales[1][:],
+                rhs=s_codes[:, cols].bitcast(FP8X4),
+                rhs_scale=s_scales[:, cols],
+                start=True,
+                stop=False,
+            )
 
         def queries_times_w1(b):
             nc.tensor.matmul_mx(
@@ -104,36 +103,37 @@ def tile_picked_recall_none_e_kernel(
                 stop=True,
             )
 
-        def interleave(copy, b, c0, c1):
-            copy(out=x_packed[b][:, c0:c1, :], in_=x_raw[b][:, :, c0:c1].rearrange("p t n -> p n t"))
+        def interleave(copy, b):
+            copy(out=x_packed[b][:], in_=x_raw[b][:].rearrange("p t n -> p n t"))
 
-        def store(b):
-            nc.sync.dma_start(out=out[:, b * BLOCK : (b + 1) * BLOCK], in_=result[b][:])
+        def take_out(copy, b):
+            j0, n = BLOCKS[b]
+            copy(out=result[b][:], in_=acc[b][:])
+            nc.sync.dma_start(out=out[:, j0 : j0 + n], in_=result[b][:])
 
-        for t in range(PACK - 1):
-            for h in range(2):
-                gather(t, h)
-        gather(3, 0)
-        interleave(nc.scalar.copy, 0, 0, BLOCK)
-        quantize(s_packed[0], s_codes[0], s_scales[0])
+        for t in range(PACK):
+            gather(t)
+        for b in range(4):
+            interleave(nc.scalar.copy, b)
+        quantize_queries(0)
+        quantize_memories(0, 512)
         memories_times_w2(0)
-        gather(3, 1)
-        interleave(nc.scalar.copy, 1, 0, BLOCK)
-        quantize(x_packed[0], x_codes[0], x_scales[0])
-        queries_times_w1(0)
-        quantize(s_packed[1], s_codes[1], s_scales[1])
         memories_times_w2(1)
-        quantize(x_packed[1], x_codes[1], x_scales[1])
+        queries_times_w1(0)
+        quantize_memories(512, 1024)
+        for b in range(2, 5):
+            memories_times_w2(b)
+        quantize_queries(1)
         queries_times_w1(1)
-        interleave(nc.scalar.copy, 2, 0, BLOCK)
-        nc.vector.tensor_copy(out=result[0][:], in_=acc[0][:])
-        store(0)
-        quantize(x_packed[2], x_codes[2], x_scales[2])
+        quantize_queries(2)
         queries_times_w1(2)
-        interleave(nc.vector.tensor_copy, 3, 0, V_COLS)
-        interleave(nc.scalar.copy, 3, V_COLS, BLOCK)
-        quantize(x_packed[3], x_codes[3], x_scales[3])
+        interleave(nc.vector.tensor_copy, 4)
+        quantize_queries(3)
         queries_times_w1(3)
-        for b in range(1, 4):
-            nc.scalar.copy(out=result[b][:], in_=acc[b][:])
-            store(b)
+        quantize_queries(4)
+        queries_times_w1(4)
+        take_out(nc.scalar.copy, 0)
+        take_out(nc.vector.tensor_copy, 1)
+        take_out(nc.scalar.copy, 2)
+        take_out(nc.vector.tensor_copy, 3)
+        take_out(nc.scalar.copy, 4)

@@ -45,7 +45,7 @@ def tile_picked_recall_none_e_kernel(
             nc.gpsimd.memset(plane[:].bitcast(I32), 0)
         for plane, scales in zip(w_scales, (w1_scales, w2_scales)):
             for q in range(4):
-                nc.scalar.dma_start(
+                nc.gpsimd.dma_start(
                     out=plane[32 * q : 32 * q + 4, :].bitcast(I32),
                     in_=scales[0, 4 * q : 4 * q + 4, :].bitcast(I32),
                 )

@@ -16,6 +16,7 @@ T = 4096
 S = 1024
 M = 128
 LISTED = 16
+LOAD = 256
 BLOCKS = ((0, 256), (256, 256), (512, 256), (768, 128), (896, 128))
 
 FLOPS = 2 * 2 * 512 * M * S
@@ -34,28 +35,42 @@ def tile_picked_recall_none_e_kernel(
 
         planes = [keep.tile([P, T], F32, name=f"plane{t}") for t in range(PACK)]
         offsets = keep.tile([P, S // LISTED], U16, name="offsets")
-        nc.sync.dma_start(out=planes[0][:], in_=s_rows[:, 0, :])
-        nc.sync.dma_start(out=offsets[:], in_=offs)
         w_codes = [keep.tile([P, M], U32, name=f"w_codes{i}", align_bytes=64) for i in range(2)]
-        for codes, words in zip(w_codes, (w1_words, w2_words)):
-            nc.sync.dma_start(out=codes[:].bitcast(I32), in_=words[0].rearrange("p m r -> p (m r)").bitcast(I32))
-        nc.sync.dma_start(out=planes[1][:], in_=s_rows[:, 1, :])
         w_scales = [keep.tile([P, M], U8, name=f"w_scales{i}", align_bytes=64) for i in range(2)]
-        for plane in w_scales:
-            nc.gpsimd.memset(plane[:].bitcast(I32), 0)
-        for plane, scales in zip(w_scales, (w1_scales, w2_scales)):
+        x_raw = [keep.tile([P, PACK, LOAD], F32, name=f"x_raw{i}") for i in range(S // LOAD)]
+
+        def load_plane(t):
+            nc.sync.dma_start(out=planes[t][:], in_=s_rows[:, t, :])
+
+        def load_codes(i):
+            words = (w1_words, w2_words)[i]
+            nc.sync.dma_start(out=w_codes[i][:].bitcast(I32), in_=words[0].rearrange("p m r -> p (m r)").bitcast(I32))
+
+        def load_scales(i):
+            scales = (w1_scales, w2_scales)[i]
             for q in range(4):
                 nc.gpsimd.dma_start(
-                    out=plane[32 * q : 32 * q + 4, :].bitcast(I32),
+                    out=w_scales[i][32 * q : 32 * q + 4, :].bitcast(I32),
                     in_=scales[0, 4 * q : 4 * q + 4, :].bitcast(I32),
                 )
-        for t in range(2, PACK):
-            nc.sync.dma_start(out=planes[t][:], in_=s_rows[:, t, :])
-        x_raw = []
-        for b, (j0, n) in enumerate(BLOCKS):
-            raw = keep.tile([P, PACK, n], F32, name=f"x_raw{b}")
-            nc.sync.dma_start(out=raw[:], in_=x_rows[:, :, j0 : j0 + n])
-            x_raw.append(raw)
+
+        def load_queries(i):
+            nc.sync.dma_start(out=x_raw[i][:], in_=x_rows[:, :, i * LOAD : (i + 1) * LOAD])
+
+        for plane in w_scales:
+            nc.gpsimd.memset(plane[:].bitcast(I32), 0)
+        load_scales(1)
+        load_scales(0)
+        load_plane(0)
+        nc.sync.dma_start(out=offsets[:], in_=offs)
+        load_plane(1)
+        load_plane(2)
+        load_plane(3)
+        load_queries(0)
+        load_codes(1)
+        load_codes(0)
+        for i in range(1, S // LOAD):
+            load_queries(i)
 
         acc = [psum.tile([P, n], F32, name=f"acc{b}") for b, (j0, n) in enumerate(BLOCKS)]
 
@@ -65,7 +80,7 @@ def tile_picked_recall_none_e_kernel(
         x_packed = [keep.tile([P, n, PACK], BF16, name=f"x_packed{b}", align_bytes=64) for b, (j0, n) in enumerate(BLOCKS)]
         x_codes = [keep.tile([P, n], U32, name=f"x_codes{b}", align_bytes=64) for b, (j0, n) in enumerate(BLOCKS)]
         x_scales = [keep.tile([P, n], U8, name=f"x_scales{b}", align_bytes=64) for b, (j0, n) in enumerate(BLOCKS)]
-        result = [keep.tile([P, n], F32, name=f"result{b}") for b, (j0, n) in enumerate(BLOCKS)]
+        result = [keep.tile([P, LOAD], F32, name=f"result{i}") for i in range(S // LOAD)]
 
         def gather(t):
             nc.vector.tensor_copy(out=s_packed[:, :, t], in_=planes[t][:].indirect(offsets[:]))
@@ -104,22 +119,31 @@ def tile_picked_recall_none_e_kernel(
             )
 
         def interleave(copy, b):
-            copy(out=x_packed[b][:], in_=x_raw[b][:].rearrange("p t n -> p n t"))
+            j0, n = BLOCKS[b]
+            cols = slice(j0 % LOAD, j0 % LOAD + n)
+            copy(
+                out=x_packed[b][:].rearrange("p (c i) t -> p c t i", i=4),
+                in_=x_raw[j0 // LOAD][:, :, cols].rearrange("p t (c i) -> p c t i", i=4),
+            )
 
         def take_out(copy, b):
             j0, n = BLOCKS[b]
-            copy(out=result[b][:], in_=acc[b][:])
-            nc.sync.dma_start(out=out[:, j0 : j0 + n], in_=result[b][:])
+            copy(out=result[j0 // LOAD][:, j0 % LOAD : j0 % LOAD + n], in_=acc[b][:])
+
+        def store(i):
+            nc.sync.dma_start(out=out[:, i * LOAD : (i + 1) * LOAD], in_=result[i][:])
 
         for t in range(PACK):
             gather(t)
-        for b in range(4):
+        for b in range(3):
             interleave(nc.scalar.copy, b)
         quantize_queries(0)
         quantize_memories(0, 512)
         memories_times_w2(0)
-        memories_times_w2(1)
         queries_times_w1(0)
+        take_out(nc.scalar.copy, 0)
+        store(0)
+        memories_times_w2(1)
         quantize_memories(512, 1024)
         for b in range(2, 5):
             memories_times_w2(b)
@@ -127,13 +151,16 @@ def tile_picked_recall_none_e_kernel(
         queries_times_w1(1)
         quantize_queries(2)
         queries_times_w1(2)
-        interleave(nc.vector.tensor_copy, 4)
-        quantize_queries(3)
-        queries_times_w1(3)
+        interleave(nc.vector.tensor_copy, 3)
+        interleave(nc.scalar.copy, 4)
         quantize_queries(4)
         queries_times_w1(4)
-        take_out(nc.scalar.copy, 0)
-        take_out(nc.vector.tensor_copy, 1)
+        quantize_queries(3)
+        queries_times_w1(3)
+        take_out(nc.scalar.copy, 1)
+        store(1)
         take_out(nc.scalar.copy, 2)
+        store(2)
+        take_out(nc.vector.tensor_copy, 4)
         take_out(nc.vector.tensor_copy, 3)
-        take_out(nc.scalar.copy, 4)
+        store(3)

from contextlib import ExitStack

import concourse.mybir as mybir

F32 = mybir.dt.float32
BF16 = mybir.dt.bfloat16
I32 = mybir.dt.int32
U32 = mybir.dt.uint32
U16 = mybir.dt.uint16
U8 = mybir.dt.uint8
FP8X4 = mybir.dt.float8_e4m3fn_x4

P = 128
PACK = 4
T = 4096
S = 1024
M = 128
LISTED = 16
LOAD = 256
BLOCKS = ((0, 256), (256, 256), (512, 256), (768, 128), (896, 128))

FLOPS = 2 * 2 * 512 * M * S


def tile_picked_recall_none_e_kernel(
    tc, xT, sT, w1_words, w1_scales, w2_words, w2_scales, offs, out
):
    nc = tc.nc
    with ExitStack() as ctx:
        keep = ctx.enter_context(tc.tile_pool(name="keep", bufs=1))
        psum = ctx.enter_context(tc.psum_pool(name="psum", bufs=1))

        s_rows = sT.rearrange("(p t) n -> p t n", t=PACK)
        x_rows = xT.rearrange("(p t) n -> p t n", t=PACK)

        planes = [keep.tile([P, T], F32, name=f"plane{t}") for t in range(PACK)]
        offsets = keep.tile([P, S // LISTED], U16, name="offsets")
        w_codes = [keep.tile([P, M], U32, name=f"w_codes{i}", align_bytes=64) for i in range(2)]
        w_scales = [keep.tile([P, M], U8, name=f"w_scales{i}", align_bytes=64) for i in range(2)]
        x_raw = [keep.tile([P, PACK, LOAD], F32, name=f"x_raw{i}") for i in range(S // LOAD)]

        def load_plane(t):
            nc.sync.dma_start(out=planes[t][:], in_=s_rows[:, t, :])

        def load_codes(i):
            words = (w1_words, w2_words)[i]
            nc.sync.dma_start(out=w_codes[i][:].bitcast(I32), in_=words[0].rearrange("p m r -> p (m r)").bitcast(I32))

        def load_scales(i):
            scales = (w1_scales, w2_scales)[i]
            for q in range(4):
                nc.gpsimd.dma_start(
                    out=w_scales[i][32 * q : 32 * q + 4, :].bitcast(I32),
                    in_=scales[0, 4 * q : 4 * q + 4, :].bitcast(I32),
                )

        def load_queries(i):
            nc.sync.dma_start(out=x_raw[i][:], in_=x_rows[:, :, i * LOAD : (i + 1) * LOAD])

        for plane in w_scales:
            nc.gpsimd.memset(plane[:].bitcast(I32), 0)
        load_scales(1)
        load_scales(0)
        load_plane(0)
        nc.sync.dma_start(out=offsets[:], in_=offs)
        load_plane(1)
        load_plane(2)
        load_plane(3)
        load_queries(0)
        load_codes(1)
        load_codes(0)
        for i in range(1, S // LOAD):
            load_queries(i)

        acc = [psum.tile([P, n], F32, name=f"acc{b}") for b, (j0, n) in enumerate(BLOCKS)]

        s_packed = keep.tile([P, S, PACK], BF16, align_bytes=64)
        s_codes = keep.tile([P, S], U32, align_bytes=64)
        s_scales = keep.tile([P, S], U8, align_bytes=64)
        x_packed = [keep.tile([P, n, PACK], BF16, name=f"x_packed{b}", align_bytes=64) for b, (j0, n) in enumerate(BLOCKS)]
        x_codes = [keep.tile([P, n], U32, name=f"x_codes{b}", align_bytes=64) for b, (j0, n) in enumerate(BLOCKS)]
        x_scales = [keep.tile([P, n], U8, name=f"x_scales{b}", align_bytes=64) for b, (j0, n) in enumerate(BLOCKS)]
        result = [keep.tile([P, LOAD], F32, name=f"result{i}") for i in range(S // LOAD)]

        def gather(t):
            nc.vector.tensor_copy(out=s_packed[:, :, t], in_=planes[t][:].indirect(offsets[:]))

        def quantize(packed, codes, scales):
            nc.vector.quantize_mx(out=codes.bitcast(FP8X4), scales=scales, in_=packed.rearrange("p n t -> p (n t)"))

        def quantize_queries(b):
            quantize(x_packed[b][:], x_codes[b][:], x_scales[b][:])

        def quantize_memories(j0, j1):
            quantize(s_packed[:, j0:j1, :], s_codes[:, j0:j1], s_scales[:, j0:j1])

        def memories_times_w2(b):
            j0, n = BLOCKS[b]
            cols = slice(j0, j0 + n)
            nc.tensor.matmul_mx(
                out=acc[b][:],
                lhsT=w_codes[1][:].bitcast(FP8X4),
                lhsT_scale=w_scales[1][:],
                rhs=s_codes[:, cols].bitcast(FP8X4),
                rhs_scale=s_scales[:, cols],
                start=True,
                stop=False,
            )

        def queries_times_w1(b):
            nc.tensor.matmul_mx(
                out=acc[b][:],
                lhsT=w_codes[0][:].bitcast(FP8X4),
                lhsT_scale=w_scales[0][:],
                rhs=x_codes[b][:].bitcast(FP8X4),
                rhs_scale=x_scales[b][:],
                start=False,
                stop=True,
            )

        def interleave(copy, b):
            j0, n = BLOCKS[b]
            cols = slice(j0 % LOAD, j0 % LOAD + n)
            copy(
                out=x_packed[b][:].rearrange("p (c i) t -> p c t i", i=4),
                in_=x_raw[j0 // LOAD][:, :, cols].rearrange("p t (c i) -> p c t i", i=4),
            )

        def take_out(copy, b):
            j0, n = BLOCKS[b]
            copy(out=result[j0 // LOAD][:, j0 % LOAD : j0 % LOAD + n], in_=acc[b][:])

        def store(i):
            nc.sync.dma_start(out=out[:, i * LOAD : (i + 1) * LOAD], in_=result[i][:])

        for t in range(PACK):
            gather(t)
        for b in range(3):
            interleave(nc.scalar.copy, b)
        quantize_queries(0)
        quantize_memories(0, 512)
        memories_times_w2(0)
        queries_times_w1(0)
        take_out(nc.scalar.copy, 0)
        store(0)
        memories_times_w2(1)
        quantize_memories(512, 1024)
        for b in range(2, 5):
            memories_times_w2(b)
        quantize_queries(1)
        queries_times_w1(1)
        quantize_queries(2)
        queries_times_w1(2)
        interleave(nc.vector.tensor_copy, 3)
        interleave(nc.scalar.copy, 4)
        quantize_queries(4)
        queries_times_w1(4)
        quantize_queries(3)
        queries_times_w1(3)
        take_out(nc.scalar.copy, 1)
        store(1)
        take_out(nc.scalar.copy, 2)
        store(2)
        take_out(nc.vector.tensor_copy, 4)
        take_out(nc.vector.tensor_copy, 3)
        store(3)
